import numpy as np
import ml_dtypes

BF16 = ml_dtypes.bfloat16


def bf(x):
    return np.asarray(x, np.float32).astype(BF16)


def f32(x):
    return np.asarray(x, np.float32)


def f64(x):
    return np.asarray(x).astype(np.float64)


def striped(idx):
    return np.concatenate([l.reshape(-1, 16).T for l in idx])


def rows(idx, k):
    return np.tile(np.repeat(idx, 16, axis=0), (k // (16 * 8), 1))


def look(tab, idx):
    return np.take_along_axis(f64(tab), rows(idx, len(tab)), axis=1)


P, K, S, V, N = 128, 256, 2048, 1536, 1536


def setup_inputs():
    return {"tab": f32(np.random.standard_normal((2, K, S))), "q": f32(0.5 * np.random.standard_normal((K, 1))), "e": bf(np.repeat(np.eye(8), 16, axis=0)), "et": bf(np.repeat(np.eye(8), 16, axis=0).T), "offs": striped(np.stack([np.random.permutation(S)[:N] for _ in range(8)]))}


def reference(tab, q, e, et, offs):
    idx = np.stack([g.T.reshape(-1) for g in np.split(offs, 8)])
    k = f64(q) * look(tab[0], idx)
    s = np.concatenate([f64(e).T @ k[a:a + P] for a in range(0, K, P)])
    p = np.exp(4.0 * np.tanh(s / 4.0))
    p = p / p.sum(axis=1, keepdims=True)
    p = np.concatenate([f64(et).T @ p[a:a + 8] for a in range(0, len(p), 8)])
    x = (p * look(tab[1], idx)).sum(axis=1).reshape(-1, P)
    return x

@@ -1,0 +1,116 @@
+import concourse.mybir as mybir
+
+F32, BF16, U16 = mybir.dt.float32, mybir.dt.bfloat16, mybir.dt.uint16
+MULT, ADD = mybir.AluOpType.mult, mybir.AluOpType.add
+ACT = mybir.ActivationFunctionType
+
+P = 128
+HEADS, HEAD_ROWS = 8, 16
+PIECE = 512
+SQUARE = 32
+CAP = 4.0
+
+FLOPS = 2 * 2 * 256 * 1536
+
+
+def tile_lookup_hattn_cap_out_kernel(tc, tab, q, e, et, offs, out):
+    nc = tc.nc
+    blocks, places = tab.shape[1] // P, tab.shape[2]
+    entries = offs.shape[1] * HEAD_ROWS
+    pieces = entries // PIECE
+    last_block = blocks - 1
+
+    with (
+        tc.tile_pool(name="held", bufs=1) as held,
+        tc.psum_pool(name="psum", bufs=1) as psum,
+    ):
+        keys = [held.tile([P, places], F32, name=f"keys{a}") for a in range(blocks)]
+        values = [held.tile([P, places], F32, name=f"values{a}") for a in range(blocks)]
+        offsets = held.tile([P, entries // HEAD_ROWS], U16, name="offsets")
+        nc.sync.dma_start(keys[0][:], tab[0, 0:P, :])
+        nc.sync.dma_start(offsets[:], offs)
+        for a in range(1, blocks):
+            nc.sync.dma_start(keys[a][:], tab[0, a * P : (a + 1) * P, :])
+        for a in range(blocks):
+            nc.sync.dma_start(values[a][:], tab[1, a * P : (a + 1) * P, :])
+
+        query = [held.tile([P, 1], F32, name=f"query{a}") for a in range(blocks)]
+        for a in range(blocks):
+            nc.scalar.dma_start(query[a][:], q[a * P : (a + 1) * P, :])
+        head_of_row = held.tile([P, HEADS], BF16, name="head_of_row")
+        nc.scalar.dma_start(head_of_row[:], e)
+
+        same_head = held.tile([P, HEADS, HEAD_ROWS], F32, name="same_head")
+        nc.vector.tensor_copy(same_head[:], head_of_row[:].unsqueeze(2).to_broadcast([P, HEADS, HEAD_ROWS]))
+        zero = held.tile([P, 1], F32, name="zero")
+        nc.vector.memset(zero[:], 0.0)
+        result = held.tile([P, SQUARE], F32, name="result", align_bytes=64)
+        nc.vector.memset(result[:], 0.0)
+
+        def piece_of_list(c):
+            columns = PIECE // HEAD_ROWS
+            return offsets[:, c * columns : (c + 1) * columns]
+
+        weight = [[held.tile([P, PIECE], F32, name=f"weight{a}_{c}") for c in range(pieces)] for a in range(blocks)]
+        total = held.tile([P, blocks], F32, name="total")
+        for a in range(blocks):
+            piece_total = held.tile([P, pieces], F32, name=f"piece_total{a}")
+            for c in range(pieces):
+                product = held.tile([P, PIECE], F32, name=f"product{a}_{c}")
+                nc.vector.tensor_scalar(
+                    product[:], keys[a][:].indirect(piece_of_list(c)), query[a][:], zero[:], MULT, ADD
+                )
+                score = psum.tile([P, PIECE], F32, name=f"score{a}_{c}")
+                nc.tensor.matmul(score[:], same_head[:].rearrange("p h r -> p (h r)"), product[:])
+                capped = held.tile([P, PIECE], F32, name=f"capped{a}_{c}")
+                nc.scalar.activation(capped[:], score[:], ACT.Tanh, scale=1.0 / CAP)
+                nc.scalar.activation(
+                    weight[a][c][:], capped[:], ACT.Exp, scale=CAP, accum_out=piece_total[:, c : c + 1]
+                )
+            summed = held.tile([P, pieces], F32, name=f"summed{a}")
+            nc.scalar.activation(summed[:], piece_total[:], ACT.Copy, accum_out=total[:, a : a + 1])
+
+        weighted = [held.tile([P, entries], F32, name=f"weighted{a}") for a in range(blocks)]
+        inverse = held.tile([P, blocks], F32, name="inverse")
+        for a in range(blocks):
+            if a == last_block:
+                nc.vector.reciprocal(inverse[:], total[:])
+            for c in range(pieces):
+                nc.vector.tensor_tensor(
+                    weighted[a][:, c * PIECE : (c + 1) * PIECE],
+                    values[a][:].indirect(piece_of_list(c)),
+                    weight[a][c][:],
+                    MULT,
+                )
+
+        scaled = held.tile([P, entries], F32, name="scaled")
+        for a in range(last_block):
+            nc.scalar.activation(
+                scaled[:], weighted[a][:], ACT.Copy, scale=inverse[:, a : a + 1], accum_out=result[:, a : a + 1]
+            )
+        before_last = entries - PIECE
+        last_inverse = inverse[:, last_block : last_block + 1]
+        partial = held.tile([P, 1], F32, name="partial")
+        nc.scalar.activation(
+            scaled[:, :before_last],
+            weighted[last_block][:, :before_last],
+            ACT.Copy,
+            scale=last_inverse,
+            accum_out=partial[:],
+        )
+        scaled_last = held.tile([P, PIECE], F32, name="scaled_last")
+        nc.vector.tensor_scalar(
+            scaled_last[:],
+            weighted[last_block][:, before_last:],
+            last_inverse,
+            partial[:],
+            MULT,
+            ADD,
+            accum_out=result[:, last_block : last_block + 1],
+        )
+
+        rows = held.tile([P, SQUARE], F32, name="rows", align_bytes=64)
+        nc.vector.transpose(rows[:], result[:])
+        for a in range(blocks):
+            queue = nc.sync if a % 2 else nc.scalar
+            queue.dma_start(out[a].rearrange("(b r) -> b r", r=SQUARE), rows[a:P:SQUARE, :])

@@ -27,21 +27,20 @@ def tile_lookup_hattn_cap_out_kernel(tc, tab, q, e, et, offs, out):
         keys = [held.tile([P, places], F32, name=f"keys{a}") for a in range(blocks)]
         values = [held.tile([P, places], F32, name=f"values{a}") for a in range(blocks)]
         offsets = held.tile([P, entries // HEAD_ROWS], U16, name="offsets")
+        query = [held.tile([P, 1], F32, name=f"query{a}") for a in range(blocks)]
+        head_of_row = held.tile([P, HEADS], BF16, name="head_of_row")
         nc.sync.dma_start(keys[0][:], tab[0, 0:P, :])
         nc.sync.dma_start(offsets[:], offs)
+        nc.sync.dma_start(query[0][:], q[0:P, :])
+        nc.sync.dma_start(head_of_row[:], e)
         for a in range(1, blocks):
+            nc.sync.dma_start(query[a][:], q[a * P : (a + 1) * P, :])
             nc.sync.dma_start(keys[a][:], tab[0, a * P : (a + 1) * P, :])
         for a in range(blocks):
             nc.sync.dma_start(values[a][:], tab[1, a * P : (a + 1) * P, :])
 
-        query = [held.tile([P, 1], F32, name=f"query{a}") for a in range(blocks)]
-        for a in range(blocks):
-            nc.scalar.dma_start(query[a][:], q[a * P : (a + 1) * P, :])
-        head_of_row = held.tile([P, HEADS], BF16, name="head_of_row")
-        nc.scalar.dma_start(head_of_row[:], e)
-
         same_head = held.tile([P, HEADS, HEAD_ROWS], F32, name="same_head")
-        nc.vector.tensor_copy(same_head[:], head_of_row[:].unsqueeze(2).to_broadcast([P, HEADS, HEAD_ROWS]))
+        nc.scalar.copy(same_head[:], head_of_row[:].unsqueeze(2).to_broadcast([P, HEADS, HEAD_ROWS]))
         zero = held.tile([P, 1], F32, name="zero")
         nc.vector.memset(zero[:], 0.0)
         result = held.tile([P, SQUARE], F32, name="result", align_bytes=64)
@@ -52,7 +51,7 @@ def tile_lookup_hattn_cap_out_kernel(tc, tab, q, e, et, offs, out):
             return offsets[:, c * columns : (c + 1) * columns]
 
         weight = [[held.tile([P, PIECE], F32, name=f"weight{a}_{c}") for c in range(pieces)] for a in range(blocks)]
-        total = held.tile([P, blocks], F32, name="total")
+        total = [held.tile([P, 1], F32, name=f"total{a}") for a in range(blocks)]
         for a in range(blocks):
             piece_total = held.tile([P, pieces], F32, name=f"piece_total{a}")
             for c in range(pieces):
@@ -68,46 +67,31 @@ def tile_lookup_hattn_cap_out_kernel(tc, tab, q, e, et, offs, out):
                     weight[a][c][:], capped[:], ACT.Exp, scale=CAP, accum_out=piece_total[:, c : c + 1]
                 )
             summed = held.tile([P, pieces], F32, name=f"summed{a}")
-            nc.scalar.activation(summed[:], piece_total[:], ACT.Copy, accum_out=total[:, a : a + 1])
+            nc.scalar.activation(summed[:], piece_total[:], ACT.Copy, accum_out=total[a][:])
 
-        weighted = [held.tile([P, entries], F32, name=f"weighted{a}") for a in range(blocks)]
-        inverse = held.tile([P, blocks], F32, name="inverse")
+        carrier = held.tile([P, PIECE + 1], F32, name="carrier")
+        last_carrier = held.tile([P, PIECE + 1], F32, name="last_carrier")
         for a in range(blocks):
-            if a == last_block:
-                nc.vector.reciprocal(inverse[:], total[:])
+            inverse = held.tile([P, 1], F32, name=f"inverse{a}")
+            nc.vector.reciprocal(inverse[:], total[a][:])
+            weighted = [held.tile([P, PIECE + 1], F32, name=f"weighted{a}_{c}") for c in range(pieces)]
             for c in range(pieces):
                 nc.vector.tensor_tensor(
-                    weighted[a][:, c * PIECE : (c + 1) * PIECE],
-                    values[a][:].indirect(piece_of_list(c)),
-                    weight[a][c][:],
-                    MULT,
+                    weighted[c][:, :PIECE], values[a][:].indirect(piece_of_list(c)), weight[a][c][:], MULT
                 )
-
-        scaled = held.tile([P, entries], F32, name="scaled")
-        for a in range(last_block):
-            nc.scalar.activation(
-                scaled[:], weighted[a][:], ACT.Copy, scale=inverse[:, a : a + 1], accum_out=result[:, a : a + 1]
-            )
-        before_last = entries - PIECE
-        last_inverse = inverse[:, last_block : last_block + 1]
-        partial = held.tile([P, 1], F32, name="partial")
-        nc.scalar.activation(
-            scaled[:, :before_last],
-            weighted[last_block][:, :before_last],
-            ACT.Copy,
-            scale=last_inverse,
-            accum_out=partial[:],
-        )
-        scaled_last = held.tile([P, PIECE], F32, name="scaled_last")
-        nc.vector.tensor_scalar(
-            scaled_last[:],
-            weighted[last_block][:, before_last:],
-            last_inverse,
-            partial[:],
-            MULT,
-            ADD,
-            accum_out=result[:, last_block : last_block + 1],
-        )
+                width = PIECE if c == 0 else PIECE + 1
+                if c < pieces - 1:
+                    nc.scalar.activation(
+                        carrier[:, :width], weighted[c][:, :width], ACT.Copy, accum_out=weighted[c + 1][:, PIECE:]
+                    )
+                elif a < last_block:
+                    nc.scalar.activation(
+                        carrier[:], weighted[c][:], ACT.Copy, scale=inverse[:], accum_out=result[:, a : a + 1]
+                    )
+                else:
+                    nc.vector.tensor_scalar(
+                        last_carrier[:], weighted[c][:], inverse[:], None, MULT, ADD, accum_out=result[:, a : a + 1]
+                    )
 
         rows = held.tile([P, SQUARE], F32, name="rows", align_bytes=64)
         nc.vector.transpose(rows[:], result[:])

@@ -9,6 +9,7 @@ HEADS, HEAD_ROWS = 8, 16
 PIECE = 512
 SQUARE = 32
 CAP = 4.0
+WARM_UP = 12
 
 FLOPS = 2 * 2 * 256 * 1536
 
@@ -38,6 +39,12 @@ def tile_lookup_hattn_cap_out_kernel(tc, tab, q, e, et, offs, out):
             nc.sync.dma_start(keys[a][:], tab[0, a * P : (a + 1) * P, :])
         for a in range(blocks):
             nc.sync.dma_start(values[a][:], tab[1, a * P : (a + 1) * P, :])
+
+        idle = held.tile([P, PIECE], BF16, name="idle")
+        nc.gpsimd.memset(idle[:], 0.0)
+        warm = psum.tile([P, PIECE], F32, name="warm")
+        for step in range(WARM_UP):
+            nc.tensor.matmul(warm[:], idle[:, :P], idle[:])
 
         same_head = held.tile([P, HEADS, HEAD_ROWS], F32, name="same_head")
         nc.scalar.copy(same_head[:], head_of_row[:].unsqueeze(2).to_broadcast([P, HEADS, HEAD_ROWS]))

import concourse.mybir as mybir

F32, BF16, U16 = mybir.dt.float32, mybir.dt.bfloat16, mybir.dt.uint16
MULT, ADD = mybir.AluOpType.mult, mybir.AluOpType.add
ACT = mybir.ActivationFunctionType

P = 128
HEADS, HEAD_ROWS = 8, 16
PIECE = 512
SQUARE = 32
CAP = 4.0
WARM_UP = 12

FLOPS = 2 * 2 * 256 * 1536


def tile_lookup_hattn_cap_out_kernel(tc, tab, q, e, et, offs, out):
    nc = tc.nc
    blocks, places = tab.shape[1] // P, tab.shape[2]
    entries = offs.shape[1] * HEAD_ROWS
    pieces = entries // PIECE
    last_block = blocks - 1

    with (
        tc.tile_pool(name="held", bufs=1) as held,
        tc.psum_pool(name="psum", bufs=1) as psum,
    ):
        keys = [held.tile([P, places], F32, name=f"keys{a}") for a in range(blocks)]
        values = [held.tile([P, places], F32, name=f"values{a}") for a in range(blocks)]
        offsets = held.tile([P, entries // HEAD_ROWS], U16, name="offsets")
        query = [held.tile([P, 1], F32, name=f"query{a}") for a in range(blocks)]
        head_of_row = held.tile([P, HEADS], BF16, name="head_of_row")
        nc.sync.dma_start(keys[0][:], tab[0, 0:P, :])
        nc.sync.dma_start(offsets[:], offs)
        nc.sync.dma_start(query[0][:], q[0:P, :])
        nc.sync.dma_start(head_of_row[:], e)
        for a in range(1, blocks):
            nc.sync.dma_start(query[a][:], q[a * P : (a + 1) * P, :])
            nc.sync.dma_start(keys[a][:], tab[0, a * P : (a + 1) * P, :])
        for a in range(blocks):
            nc.sync.dma_start(values[a][:], tab[1, a * P : (a + 1) * P, :])

        idle = held.tile([P, PIECE], BF16, name="idle")
        nc.gpsimd.memset(idle[:], 0.0)
        warm = psum.tile([P, PIECE], F32, name="warm")
        for step in range(WARM_UP):
            nc.tensor.matmul(warm[:], idle[:, :P], idle[:])

        same_head = held.tile([P, HEADS, HEAD_ROWS], F32, name="same_head")
        nc.scalar.copy(same_head[:], head_of_row[:].unsqueeze(2).to_broadcast([P, HEADS, HEAD_ROWS]))
        zero = held.tile([P, 1], F32, name="zero")
        nc.vector.memset(zero[:], 0.0)
        result = held.tile([P, SQUARE], F32, name="result", align_bytes=64)
        nc.vector.memset(result[:], 0.0)

        def piece_of_list(c):
            columns = PIECE // HEAD_ROWS
            return offsets[:, c * columns : (c + 1) * columns]

        weight = [[held.tile([P, PIECE], F32, name=f"weight{a}_{c}") for c in range(pieces)] for a in range(blocks)]
        total = [held.tile([P, 1], F32, name=f"total{a}") for a in range(blocks)]
        for a in range(blocks):
            piece_total = held.tile([P, pieces], F32, name=f"piece_total{a}")
            for c in range(pieces):
                product = held.tile([P, PIECE], F32, name=f"product{a}_{c}")
                nc.vector.tensor_scalar(
                    product[:], keys[a][:].indirect(piece_of_list(c)), query[a][:], zero[:], MULT, ADD
                )
                score = psum.tile([P, PIECE], F32, name=f"score{a}_{c}")
                nc.tensor.matmul(score[:], same_head[:].rearrange("p h r -> p (h r)"), product[:])
                capped = held.tile([P, PIECE], F32, name=f"capped{a}_{c}")
                nc.scalar.activation(capped[:], score[:], ACT.Tanh, scale=1.0 / CAP)
                nc.scalar.activation(
                    weight[a][c][:], capped[:], ACT.Exp, scale=CAP, accum_out=piece_total[:, c : c + 1]
                )
            summed = held.tile([P, pieces], F32, name=f"summed{a}")
            nc.scalar.activation(summed[:], piece_total[:], ACT.Copy, accum_out=total[a][:])

        carrier = held.tile([P, PIECE + 1], F32, name="carrier")
        last_carrier = held.tile([P, PIECE + 1], F32, name="last_carrier")
        for a in range(blocks):
            inverse = held.tile([P, 1], F32, name=f"inverse{a}")
            nc.vector.reciprocal(inverse[:], total[a][:])
            weighted = [held.tile([P, PIECE + 1], F32, name=f"weighted{a}_{c}") for c in range(pieces)]
            for c in range(pieces):
                nc.vector.tensor_tensor(
                    weighted[c][:, :PIECE], values[a][:].indirect(piece_of_list(c)), weight[a][c][:], MULT
                )
                width = PIECE if c == 0 else PIECE + 1
                if c < pieces - 1:
                    nc.scalar.activation(
                        carrier[:, :width], weighted[c][:, :width], ACT.Copy, accum_out=weighted[c + 1][:, PIECE:]
                    )
                elif a < last_block:
                    nc.scalar.activation(
                        carrier[:], weighted[c][:], ACT.Copy, scale=inverse[:], accum_out=result[:, a : a + 1]
                    )
                else:
                    nc.vector.tensor_scalar(
                        last_carrier[:], weighted[c][:], inverse[:], None, MULT, ADD, accum_out=result[:, a : a + 1]
                    )

        rows = held.tile([P, SQUARE], F32, name="rows", align_bytes=64)
        nc.vector.transpose(rows[:], result[:])
        for a in range(blocks):
            queue = nc.sync if a % 2 else nc.scalar
            queue.dma_start(out[a].rearrange("(b r) -> b r", r=SQUARE), rows[a:P:SQUARE, :])
